import numpy as np, ml_dtypes
CORES = [0,1,2,3,4,5,6,7]
N = 8
def setup_inputs(rng):
    return {"x": rng.standard_normal((N, 128, 2048), dtype=np.float32).astype(ml_dtypes.bfloat16)}
def reference(x):
    g = np.concatenate(list(x), axis=1)
    return {"y": np.broadcast_to(g, (N,) + g.shape)}

from concourse.bass import DstId, RemoteDMATransfer

N = 8
W = 2048

SCRATCH = {
    "land": ("sbuf", [128, N * W], "bfloat16"),
}
SEMAPHORES = ["loaded", "sent", "stored"] + ["arr%d" % j for j in range(N)]


def rank_program(g, core, T, topo):
    r = T.rank_of(core)
    if r is None:
        return

    def blk(t, j):
        return t[:, j * W:(j + 1) * W]

    g.sync.dma_start(blk(T.land, r), T.x[:]).then_inc(T.sem.loaded, 16)

    peers = [(r + k) % N for k in range(1, N)]
    ids = []
    for p in peers:
        rid, pid, _se = topo.addr(T.cores[p])
        ids.append(DstId(rid=rid, pnc=pid))
    g.wait_ge(T.sem.loaded, 16)
    g.remote_dma_fused(
        [RemoteDMATransfer(dst_ids=ids, dma_engine_mask=0xFFFF, remote_sem=T.sem["arr%d" % r],
                           srcs=[blk(T.land, r)], dsts=[blk(T.land, r) for _p in peers])],
        local_sem=T.sem.sent)

    g.sync.wait_ge(T.sem.loaded, 16)
    g.sync.dma_start(blk(T.y, r), blk(T.land, r)).then_inc(T.sem.stored, 16)
    for k in range(1, N):
        j = (r - k) % N
        q = g.scalar if k % 2 else g.sync
        q.wait_ge(T.sem["arr%d" % j], 16)
        q.dma_start(blk(T.y, j), blk(T.land, j)).then_inc(T.sem.stored, 16)

    g.wait_ge(T.sem.sent, 16)
    g.wait_ge(T.sem.stored, 16 * N)
